import numpy as np
import ml_dtypes


def mxq(x, axis, fmt="e4m3"):
    dtype, down = {"e4m3": (ml_dtypes.float8_e4m3fn, 7), "e5m2": (ml_dtypes.float8_e5m2, 14)}[fmt]
    v = np.moveaxis(np.asarray(x, np.float32).astype(ml_dtypes.bfloat16).astype(np.float64), axis, -1)
    blocks = v.reshape(v.shape[:-1] + (-1, 32))
    amax = np.abs(blocks).max(-1, keepdims=True)
    byte = np.maximum(np.where(amax > 0, np.frexp(amax)[1] - 1 + 127, 0) - down, 1)
    scale = np.exp2(byte - 127.0)
    codes = (blocks / scale).astype(np.float32).astype(dtype).astype(np.float64)
    return np.moveaxis((codes * scale).reshape(v.shape), -1, axis)


WIDE = False


def mx_kscale(k):
    if not WIDE:
        return np.ones(k)
    levels = np.array([10, -10, 5, -5, 0])
    if k % 512:
        return np.exp2(np.random.permutation(np.resize(levels, k // 32))).repeat(32)
    a = np.empty((k // 512, 16))
    for p in range(k // 512):
        a[p, :8] = np.random.permutation(np.resize(levels, 8))
        for g in range(8):
            far = levels[np.abs(levels - a[p, g]) >= 10]
            a[p, g + 8] = far[np.random.randint(len(far))]
    return np.exp2(a.ravel()).repeat(32)


def f64(x):
    return np.asarray(x).astype(np.float64)


def striped(idx):
    return np.tile(idx.reshape(-1, 16).T, (8, 1)).astype(np.uint16)


def unstriped(offs):
    return offs[:16].T.reshape(-1).astype(np.int64)


def pack_weight(w):
    k, n = w.shape
    w = f64(np.asarray(w, np.float32).astype(ml_dtypes.bfloat16)).reshape(k // 32, 32, n)
    amax = np.abs(w).max(1)
    byte = np.clip(np.where(amax > 0, np.frexp(amax)[1] - 1 + 127 - 7, 1), 1, 254)
    scaled = (w * np.exp2(127.0 - byte)[:, None, :]).reshape(k, n).astype(np.float32)
    words = np.ascontiguousarray(scaled.reshape(k // 512, 128, 4, n).transpose(0, 1, 3, 2)).astype(ml_dtypes.float8_e4m3fn).view(np.uint8)
    return words, np.ascontiguousarray(byte.astype(np.uint8).reshape(k // 512, 16, n))


def unpack_weight(words, scales):
    g, p, n, _ = words.shape
    vals = np.ascontiguousarray(words).view(ml_dtypes.float8_e4m3fn).astype(np.float64) * np.repeat(np.exp2(scales.astype(np.float64) - 127.0), 8, axis=1)[..., None]
    return vals.transpose(0, 1, 3, 2).reshape(g * 512, n)


E2M1 = np.array([0.0, 0.5, 1.0, 1.5, 2.0, 3.0, 4.0, 6.0, -0.0, -0.5, -1.0, -1.5, -2.0, -3.0, -4.0, -6.0])


def pack_fp4(w):
    k, n = w.shape
    w = f64(np.asarray(w, np.float32).astype(ml_dtypes.bfloat16)).reshape(k // 32, 32, n)
    amax = np.abs(w).max(1)
    mant, ex = np.frexp(amax / 6.0)
    byte = np.clip(np.where(amax > 0, np.where(mant > 0.5, ex, ex - 1) + 127, 1), 1, 254)
    scaled = (w * np.exp2(127.0 - byte)[:, None, :]).reshape(k, n).astype(np.float32)
    c = np.ascontiguousarray(scaled.reshape(k // 512, 128, 4, n).transpose(0, 1, 3, 2)).astype(ml_dtypes.float4_e2m1fn).view(np.uint8) & 0xF
    words = (c[..., 0::2] | (c[..., 1::2] << 4)).reshape(k // 512, 128, 2 * n)
    return np.ascontiguousarray(words), np.ascontiguousarray(byte.astype(np.uint8).reshape(k // 512, 16, n))


def unpack_fp4(words, scales):
    g, _, n = scales.shape
    words = np.ascontiguousarray(words).reshape(g, 128, n, 2)
    nib = np.empty((g, 128, n, 4), np.uint8)
    nib[..., 0::2] = words & 0xF
    nib[..., 1::2] = words >> 4
    vals = E2M1[nib] * np.repeat(np.exp2(scales.astype(np.float64) - 127.0), 8, axis=1)[..., None]
    return vals.transpose(0, 1, 3, 2).reshape(g * 512, n)


def planes(y):
    n, m = y.shape
    v = y.astype(np.float32).astype(ml_dtypes.bfloat16).astype(np.float64).reshape(n // 32, 32, m)
    top = np.abs(v).max(1)
    byte = np.clip(np.where(top > 0, np.frexp(top)[1] - 1 + 127 - 7, 1), 1, 254)
    codes = (v * np.exp2(127.0 - byte)[:, None, :]).reshape(n, m).astype(np.float32).astype(ml_dtypes.float8_e4m3fn).view(np.uint8)
    words = codes.reshape(n // 512, 128, 4, m).transpose(0, 1, 3, 2)
    return np.ascontiguousarray(words), np.ascontiguousarray(byte.astype(np.uint8).reshape(n // 512, 16, m))


K, T, S, N, H, U = 512, 2048, 512, 512, 512, 1024


def setup_inputs():
    n = np.random.standard_normal
    s = mx_kscale(K)[:, None]
    u = mx_kscale(H)
    packed_xT = pack_weight(n((K, T)) * s)
    packed_w1 = pack_fp4(n((K, N)) / np.sqrt(K) / s)
    packed_w2 = pack_fp4(n((H, N)) / np.sqrt(H) / u[:, None])
    return {
        "x_words": packed_xT[0],
        "x_scales": packed_xT[1],
        "w1_words": packed_w1[0],
        "w1_scales": packed_w1[1],
        "tw": (0.6 * n((H, U))).astype(np.float32),
        "unit": (np.random.uniform(0.6, 1.4, (H, 1)) * u[:, None]).astype(np.float32),
        "w2_words": packed_w2[0],
        "w2_scales": packed_w2[1],
        "offs": striped(np.random.permutation(T)[:S]),
        "f1": striped(np.random.permutation(np.concatenate([np.arange(S), np.random.randint(0, S, U - S)]))),
        "f2": striped(np.random.permutation(np.concatenate([np.arange(S), np.random.randint(0, S, U - S)]))),
        "f3": striped(np.random.permutation(np.concatenate([np.arange(S), np.random.randint(0, S, U - S)]))),
        "f4": striped(np.random.permutation(np.concatenate([np.arange(S), np.random.randint(0, S, U - S)]))),
    }


def reference(x_words, x_scales, w1_words, w1_scales, tw, unit, w2_words, w2_scales, offs, f1, f2, f3, f4):
    xq = unpack_weight(x_words, x_scales)[:, unstriped(offs)]
    y = unpack_fp4(w1_words, w1_scales).T @ xq
    y1 = y[:, unstriped(f1)]
    y3 = y[:, unstriped(f3)]
    dia = y1 + y3
    y2 = y[:, unstriped(f2)]
    y4 = y[:, unstriped(f4)]
    dib = y2 + y4
    hid = f64(unit) * (np.maximum(dia, dib) - f64(tw))
    out_0 = unpack_fp4(w2_words, w2_scales).T @ mxq(hid, 0, "e4m3")
    return (out_0,) + planes(out_0)

@@ -1,0 +1,258 @@
+from contextlib import ExitStack
+
+import concourse.mybir as mybir
+
+K, T, S, H, U = 512, 2048, 512, 512, 1024
+FLOPS = 2 * K * H * S + 2 * H * H * U
+
+F32 = mybir.dt.float32
+BF16 = mybir.dt.bfloat16
+I32 = mybir.dt.int32
+U32 = mybir.dt.uint32
+U16 = mybir.dt.uint16
+U8 = mybir.dt.uint8
+FP8X4 = mybir.dt.float8_e4m3fn_x4
+FP4X4 = mybir.dt.float4_e2m1fn_x4
+ALU = mybir.AluOpType
+COPY = mybir.ActivationFunctionType.Copy
+
+P = 128
+PACK = 4
+BANK = 512
+STRIP = BANK // PACK
+CHUNKS = [512,384,128]
+WINDOW = max(S, max(CHUNKS)) + 16
+SCALAR_GATHERS = [[2,2,2,2],[2,2,2,2],[2,2,2,2]]
+
+
+def tile_picked_yquadfm_max_po_kernel(
+    tc, x_words, x_scales, w1_words, w1_scales, tw, unit, w2_words, w2_scales, offs, f1, f2, f3, f4, out_0, out_1, out_2
+):
+    nc = tc.nc
+    with ExitStack() as ctx:
+        keep = ctx.enter_context(tc.tile_pool(name="keep", bufs=1))
+        ring = ctx.enter_context(tc.tile_pool(name="ring", bufs=3))
+        stage = ctx.enter_context(tc.tile_pool(name="stage", bufs=2))
+        streamed = ctx.enter_context(tc.tile_pool(name="streamed", bufs=2))
+        psum = ctx.enter_context(tc.psum_pool(name="psum", bufs=8))
+
+        def load_scale_rows(queues, tile, rows):
+            for q in range(4):
+                queues[q].dma_start(out=tile[32 * q : 32 * q + 4, :].bitcast(I32), in_=rows[0, 4 * q : 4 * q + 4, :].bitcast(I32))
+
+        def deal_words(words, name):
+            dealt = keep.tile([P, 2 * H], U8, align_bytes=64, name=name)
+            nc.vector.tensor_copy(
+                out=dealt[:].rearrange("p (t m b) -> p t m b", t=PACK, b=2),
+                in_=words[:].rearrange("p (m t b) -> p t m b", t=PACK, b=2),
+            )
+            return dealt
+
+        def deal_scales(scales, name):
+            dealt = keep.tile([P, H], U8, align_bytes=64, name=name)
+            nc.vector.tensor_copy(
+                out=dealt[:].rearrange("p (t m) -> p t m", t=PACK),
+                in_=scales[:].rearrange("p (m t) -> p t m", t=PACK),
+            )
+            return dealt
+
+        def product(acc, weights, t, codes, scales):
+            words, weight_scales = weights
+            nc.tensor.matmul_mx(
+                out=acc,
+                lhsT=words[:, 2 * P * t : 2 * P * (t + 1)].bitcast(FP4X4),
+                lhsT_scale=weight_scales[:, P * t : P * (t + 1)],
+                rhs=codes.bitcast(FP8X4),
+                rhs_scale=scales,
+                start=True,
+                stop=True,
+            )
+
+        x_scale_table = streamed.tile([P, T], U8, name="streamed")
+        x_word_table = streamed.tile([P, T], I32, name="streamed")
+        weight_scale_rows = keep.tile([P, H], U8)
+        weight_words = keep.tile([P, 2 * H], U8)
+        picks = keep.tile([P, S // 16], U16)
+        corners = [keep.tile([P, U // 16], U16, name="corner_%d" % i) for i in range(4)]
+        unit_cols = keep.tile([P, PACK], F32)
+        nc.gpsimd.memset(x_scale_table[:].bitcast(I32), 0)
+        nc.vector.memset(weight_scale_rows[:].bitcast(I32), 0)
+        nc.sync.dma_start(picks[:], offs)
+        nc.sync.dma_start(out=weight_words[:].bitcast(I32), in_=w1_words[0].bitcast(I32))
+        nc.sync.dma_start(out=x_word_table[:], in_=x_words[0].rearrange("p c r -> p (c r)").bitcast(I32))
+        load_scale_rows([nc.sync] * 4, x_scale_table, x_scales)
+        load_scale_rows([nc.sync, nc.sync, nc.sync, nc.gpsimd], weight_scale_rows, w1_scales)
+        for corner, face_list in zip(corners, (f1, f2, f3, f4)):
+            nc.sync.dma_start(corner[:], face_list)
+        nc.gpsimd.dma_start(out=unit_cols[:], in_=unit.rearrange("(p t) o -> p (t o)", t=PACK))
+
+        starts = [sum(CHUNKS[:c]) for c in range(len(CHUNKS))]
+        tw_rows = tw.rearrange("(p t) r -> p t r", t=PACK)
+        targets = []
+
+        def load_target(t):
+            target = streamed.tile([P, U], F32, name="streamed")
+            nc.sync.dma_start(out=target[:], in_=tw_rows[:, t, :])
+            targets.append(target)
+
+        scaled = []
+
+        def scale_target(t):
+            rows = keep.tile([P, U], F32, name="scaled_target_%d" % t)
+            nc.scalar.activation(rows[:], targets[t][:], COPY, scale=unit_cols[:, t : t + 1])
+            scaled.append(rows)
+
+        x_code_scales = keep.tile([P, S], U8, align_bytes=64)
+        w1_dealt = deal_words(weight_words, "w1_dealt_words")
+        nc.vector.tensor_copy(x_code_scales[:], x_scale_table[:].indirect(picks[:]))
+        w1 = (w1_dealt, deal_scales(weight_scale_rows, "w1_dealt_scales"))
+        y = [keep.tile([P, WINDOW], F32, name="y_%d" % t) for t in range(PACK)]
+        for t in range(PACK):
+            nc.gpsimd.memset(y[t][:, S:], 0.0)
+        half = S // 2
+        first = {}
+        for h in range(2):
+            x_codes = keep.tile([P, half], U32, align_bytes=64, name="x_codes_%d" % h)
+            nc.vector.tensor_copy(x_codes[:], x_word_table[:].bitcast(U32).indirect(picks[:, h * half // 16 : (h + 1) * half // 16]))
+            for t in range(PACK):
+                first[h, t] = psum.tile([P, half], F32, name="acc")
+                product(first[h, t][:], w1, t, x_codes[:], x_code_scales[:, h * half : (h + 1) * half])
+        load_target(0)
+        nc.sync.dma_start(out=weight_words[:].bitcast(I32), in_=w2_words[0].bitcast(I32))
+        load_scale_rows([nc.sync] * 4, weight_scale_rows, w2_scales)
+        load_target(1)
+        for t in range(PACK):
+            for h in range(2):
+                if (h, t) in ((0, 0), (1, 0), (0, 1)):
+                    nc.scalar.activation(y[t][:, h * half : (h + 1) * half], first[h, t][:], COPY)
+                else:
+                    nc.vector.tensor_copy(out=y[t][:, h * half : (h + 1) * half], in_=first[h, t][:])
+        w2 = (deal_words(weight_words, "w2_dealt_words"), deal_scales(weight_scale_rows, "w2_dealt_scales"))
+
+        out_rows = out_0.rearrange("(p t) r -> p t r", t=PACK)
+        out_words = out_1[0].rearrange("p c r -> p (c r)").bitcast(I32)
+        plane_scales = keep.tile([P, U], U8, align_bytes=64)
+
+        fetched = {}
+        hid = {}
+        grouped = {}
+        accs = {}
+        results = {}
+        rounded = {}
+
+        def window(c, t, which):
+            r0, n = starts[c], CHUNKS[c]
+            return y[t][:].indirect(corners[which][:, r0 // 16 : (r0 + n) // 16])
+
+        def scalar_gathers(c, t):
+            n = CHUNKS[c]
+            for which in range(SCALAR_GATHERS[c][t]):
+                values = ring.tile([P, n], F32, name="fetched_%d" % which)
+                nc.scalar.activation(values[:], window(c, t, which), COPY)
+                fetched[c, t, which] = values
+
+        def diagonal(c, t, corner):
+            n = CHUNKS[c]
+            total = ring.tile([P, n], F32, name="diagonal_%d" % corner)
+            if (c, t, corner + 2) in fetched:
+                nc.vector.tensor_tensor(total[:], fetched[c, t, corner + 2][:], fetched[c, t, corner][:], ALU.add)
+            else:
+                nc.vector.tensor_tensor(total[:], window(c, t, corner + 2), fetched[c, t, corner][:], ALU.add)
+            return total
+
+        sums = {}
+        larger = {}
+
+        def add_corners(c, t):
+            sums[c, t] = (diagonal(c, t, 0), diagonal(c, t, 1))
+
+        def take_larger(c, t):
+            larger[c, t] = ring.tile([P, CHUNKS[c]], F32, name="larger")
+            nc.vector.tensor_tensor(larger[c, t][:], sums[c, t][0][:], sums[c, t][1][:], ALU.max)
+
+        def make_hid(c, t):
+            r0, n = starts[c], CHUNKS[c]
+            if t == 0:
+                hid[c] = stage.tile([P, PACK, n], BF16, name="hid")
+            nc.vector.scalar_tensor_tensor(
+                hid[c][:, t, :], larger[c, t][:], unit_cols[:, t : t + 1], scaled[t][:, r0 : r0 + n], ALU.mult, ALU.subtract
+            )
+
+        def group_hid(c):
+            grouped[c] = stage.tile([P, CHUNKS[c], PACK], BF16, align_bytes=64, name="hid_grouped")
+            nc.vector.tensor_copy(
+                out=grouped[c][:].rearrange("p (c i) t -> p c t i", i=4), in_=hid[c][:].rearrange("p t (c i) -> p c t i", i=4)
+            )
+
+        def second_product(c):
+            n = CHUNKS[c]
+            codes = stage.tile([P, n], U32, align_bytes=64, name="hid_codes")
+            scales = stage.tile([P, n], U8, align_bytes=64, name="hid_scales")
+            nc.vector.quantize_mx(out=codes[:].bitcast(FP8X4), scales=scales[:], in_=grouped[c][:].rearrange("p r t -> p (r t)"))
+            accs[c] = []
+            for b in range(n // STRIP):
+                acc = psum.tile([P, PACK, STRIP], F32, name="acc")
+                cols = slice(b * STRIP, (b + 1) * STRIP)
+                for t in range(PACK):
+                    product(acc[:, t, :], w2, t, codes[:, cols], scales[:, cols])
+                accs[c].append(acc)
+            results[c] = stage.tile([P, PACK, n], F32, name="result")
+            rounded[c] = stage.tile([P, n, PACK], BF16, align_bytes=64, name="rounded")
+
+        def empty_banks(c, banks):
+            for b in banks:
+                cols = slice(b * STRIP, (b + 1) * STRIP)
+                nc.scalar.copy(out=results[c][:, :, cols], in_=accs[c][b][:])
+                if c + 1 < len(CHUNKS):
+                    nc.scalar.copy(out=rounded[c][:, cols, :], in_=accs[c][b][:].rearrange("p t r -> p r t"))
+                else:
+                    nc.vector.tensor_copy(out=rounded[c][:, cols, :], in_=accs[c][b][:].rearrange("p t r -> p r t"))
+
+        def store_result(c):
+            r0, n = starts[c], CHUNKS[c]
+            nc.sync.dma_start(out=out_rows[:, :, r0 : r0 + n], in_=results[c][:])
+
+        def store_planes(c):
+            r0, n = starts[c], CHUNKS[c]
+            words = stage.tile([P, n], I32, align_bytes=64, name="plane_words")
+            nc.vector.quantize_mx(
+                out=words[:].bitcast(FP8X4), scales=plane_scales[:, r0 : r0 + n], in_=rounded[c][:].rearrange("p r t -> p (r t)")
+            )
+            nc.sync.dma_start(out=out_words[:, r0 : r0 + n], in_=words[:])
+
+        def after_chunk(c, step):
+            banks = list(range(CHUNKS[c] // STRIP))
+            cut = (len(banks) + 1) // 2
+            if step == 0:
+                group_hid(c)
+            elif step == 1:
+                second_product(c)
+                empty_banks(c, banks[:cut])
+            elif step == 2:
+                empty_banks(c, banks[cut:])
+                store_result(c)
+            else:
+                store_planes(c)
+
+        units = [(c, t) for c in range(len(CHUNKS)) for t in range(PACK)]
+        scalar_gathers(*units[0])
+        for i, (c, t) in enumerate(units):
+            if i + 1 < len(units):
+                scalar_gathers(*units[i + 1])
+            if c == 0:
+                scale_target(t)
+                if t + 2 < PACK:
+                    load_target(t + 2)
+            add_corners(c, t)
+            if i > 0:
+                make_hid(*units[i - 1])
+            take_larger(c, t)
+            if c > 0:
+                after_chunk(c - 1, t)
+        make_hid(*units[-1])
+        for step in range(4):
+            after_chunk(len(CHUNKS) - 1, step)
+        for q in range(4):
+            nc.scalar.dma_start(
+                out=out_2[0, 4 * q : 4 * q + 4, :].bitcast(I32), in_=plane_scales[32 * q : 32 * q + 4, :].bitcast(I32)
+            )

@@ -22,7 +22,7 @@ BANK = 512
 STRIP = BANK // PACK
 CHUNKS = [512,384,128]
 WINDOW = max(S, max(CHUNKS)) + 16
-SCALAR_GATHERS = [[2,2,2,2],[2,2,2,2],[2,2,2,2]]
+SCALAR_GATHERS = [[2,2,2,2],[2,2,2,3],[2,2,2,2]]
 
 
 def tile_picked_yquadfm_max_po_kernel(
@@ -36,9 +36,8 @@ def tile_picked_yquadfm_max_po_kernel(
         streamed = ctx.enter_context(tc.tile_pool(name="streamed", bufs=2))
         psum = ctx.enter_context(tc.psum_pool(name="psum", bufs=8))
 
-        def load_scale_rows(queues, tile, rows):
-            for q in range(4):
-                queues[q].dma_start(out=tile[32 * q : 32 * q + 4, :].bitcast(I32), in_=rows[0, 4 * q : 4 * q + 4, :].bitcast(I32))
+        def load_scale_rows(queue, plane, rows, q):
+            queue.dma_start(out=plane[32 * q : 32 * q + 4, :].bitcast(I32), in_=rows[0, 4 * q : 4 * q + 4, :].bitcast(I32))
 
         def deal_words(words, name):
             dealt = keep.tile([P, 2 * H], U8, align_bytes=64, name=name)
@@ -52,7 +51,7 @@ def tile_picked_yquadfm_max_po_kernel(
             dealt = keep.tile([P, H], U8, align_bytes=64, name=name)
             nc.vector.tensor_copy(
                 out=dealt[:].rearrange("p (t m) -> p t m", t=PACK),
-                in_=scales[:].rearrange("p (m t) -> p t m", t=PACK),
+                in_=scales.rearrange("p (m t) -> p t m", t=PACK),
             )
             return dealt
 
@@ -68,23 +67,25 @@ def tile_picked_yquadfm_max_po_kernel(
                 stop=True,
             )
 
-        x_scale_table = streamed.tile([P, T], U8, name="streamed")
+        x_scale_table = keep.tile([P, T], U8, name="x_scale_table", tag="scale_table_then_unit")
+        w1_raw = streamed.tile([P, 2 * H], U8, name="streamed")
         x_word_table = streamed.tile([P, T], I32, name="streamed")
-        weight_scale_rows = keep.tile([P, H], U8)
-        weight_words = keep.tile([P, 2 * H], U8)
+        weight_scale_rows = keep.tile([P, 2 * H], U8)
         picks = keep.tile([P, S // 16], U16)
         corners = [keep.tile([P, U // 16], U16, name="corner_%d" % i) for i in range(4)]
-        unit_cols = keep.tile([P, PACK], F32)
-        nc.gpsimd.memset(x_scale_table[:].bitcast(I32), 0)
+        nc.vector.memset(x_scale_table[:].bitcast(I32), 0)
         nc.vector.memset(weight_scale_rows[:].bitcast(I32), 0)
         nc.sync.dma_start(picks[:], offs)
-        nc.sync.dma_start(out=weight_words[:].bitcast(I32), in_=w1_words[0].bitcast(I32))
-        nc.sync.dma_start(out=x_word_table[:], in_=x_words[0].rearrange("p c r -> p (c r)").bitcast(I32))
-        load_scale_rows([nc.sync] * 4, x_scale_table, x_scales)
-        load_scale_rows([nc.sync, nc.sync, nc.sync, nc.gpsimd], weight_scale_rows, w1_scales)
         for corner, face_list in zip(corners, (f1, f2, f3, f4)):
             nc.sync.dma_start(corner[:], face_list)
-        nc.gpsimd.dma_start(out=unit_cols[:], in_=unit.rearrange("(p t) o -> p (t o)", t=PACK))
+        nc.sync.dma_start(out=w1_raw[:].bitcast(I32), in_=w1_words[0].bitcast(I32))
+        nc.sync.dma_start(out=x_word_table[:], in_=x_words[0].rearrange("p c r -> p (c r)").bitcast(I32))
+        for q in range(4):
+            load_scale_rows(nc.sync, x_scale_table[:], x_scales, q)
+        for q in range(4):
+            load_scale_rows(nc.gpsimd if q == 3 else nc.sync, weight_scale_rows[:, :H], w1_scales, q)
+        for q in range(4):
+            load_scale_rows(nc.sync, weight_scale_rows[:, H:], w2_scales, q)
 
         starts = [sum(CHUNKS[:c]) for c in range(len(CHUNKS))]
         tw_rows = tw.rearrange("(p t) r -> p t r", t=PACK)
@@ -102,32 +103,40 @@ def tile_picked_yquadfm_max_po_kernel(
             nc.scalar.activation(rows[:], targets[t][:], COPY, scale=unit_cols[:, t : t + 1])
             scaled.append(rows)
 
-        x_code_scales = keep.tile([P, S], U8, align_bytes=64)
-        w1_dealt = deal_words(weight_words, "w1_dealt_words")
-        nc.vector.tensor_copy(x_code_scales[:], x_scale_table[:].indirect(picks[:]))
-        w1 = (w1_dealt, deal_scales(weight_scale_rows, "w1_dealt_scales"))
+        w1_dealt = deal_words(w1_raw, "w1_dealt_words")
         y = [keep.tile([P, WINDOW], F32, name="y_%d" % t) for t in range(PACK)]
         for t in range(PACK):
-            nc.gpsimd.memset(y[t][:, S:], 0.0)
+            nc.vector.memset(y[t][:, S:], 0.0)
         half = S // 2
+        halves = [picks[:, h * half // 16 : (h + 1) * half // 16] for h in range(2)]
+        x_codes = [keep.tile([P, half], U32, align_bytes=64, name="x_codes_%d" % h) for h in range(2)]
+        x_code_scales = [keep.tile([P, half], U8, align_bytes=64, name="x_code_scales_%d" % h) for h in range(2)]
+        for h in range(2):
+            nc.vector.tensor_copy(x_codes[h][:], x_word_table[:].bitcast(U32).indirect(halves[h]))
+        nc.vector.tensor_copy(x_code_scales[0][:], x_scale_table[:].indirect(halves[0]))
+        w1 = (w1_dealt, deal_scales(weight_scale_rows[:, :H], "w1_dealt_scales"))
+        nc.vector.tensor_copy(x_code_scales[1][:], x_scale_table[:].indirect(halves[1]))
         first = {}
         for h in range(2):
-            x_codes = keep.tile([P, half], U32, align_bytes=64, name="x_codes_%d" % h)
-            nc.vector.tensor_copy(x_codes[:], x_word_table[:].bitcast(U32).indirect(picks[:, h * half // 16 : (h + 1) * half // 16]))
             for t in range(PACK):
                 first[h, t] = psum.tile([P, half], F32, name="acc")
-                product(first[h, t][:], w1, t, x_codes[:], x_code_scales[:, h * half : (h + 1) * half])
+                product(first[h, t][:], w1, t, x_codes[h][:], x_code_scales[h][:])
+        unit_cols = keep.tile([P, PACK], F32, name="unit_cols", tag="scale_table_then_unit")
+        nc.sync.dma_start(out=unit_cols[:], in_=unit.rearrange("(p t) o -> p (t o)", t=PACK))
+        w2_raw = streamed.tile([P, 2 * H], U8, name="streamed")
+        nc.sync.dma_start(out=w2_raw[:].bitcast(I32), in_=w2_words[0].bitcast(I32))
         load_target(0)
-        nc.sync.dma_start(out=weight_words[:].bitcast(I32), in_=w2_words[0].bitcast(I32))
-        load_scale_rows([nc.sync] * 4, weight_scale_rows, w2_scales)
-        load_target(1)
-        for t in range(PACK):
+
+        def copy_out_y(t, on_scalar):
             for h in range(2):
-                if (h, t) in ((0, 0), (1, 0), (0, 1)):
+                if on_scalar:
                     nc.scalar.activation(y[t][:, h * half : (h + 1) * half], first[h, t][:], COPY)
                 else:
                     nc.vector.tensor_copy(out=y[t][:, h * half : (h + 1) * half], in_=first[h, t][:])
-        w2 = (deal_words(weight_words, "w2_dealt_words"), deal_scales(weight_scale_rows, "w2_dealt_scales"))
+
+        copy_out_y(0, True)
+        copy_out_y(1, False)
+        w2 = (deal_words(w2_raw, "w2_dealt_words"), deal_scales(weight_scale_rows[:, H:], "w2_dealt_scales"))
 
         out_rows = out_0.rearrange("(p t) r -> p t r", t=PACK)
         out_words = out_1[0].rearrange("p c r -> p (c r)").bitcast(I32)
@@ -202,11 +211,11 @@ def tile_picked_yquadfm_max_po_kernel(
         def empty_banks(c, banks):
             for b in banks:
                 cols = slice(b * STRIP, (b + 1) * STRIP)
-                nc.scalar.copy(out=results[c][:, :, cols], in_=accs[c][b][:])
                 if c + 1 < len(CHUNKS):
                     nc.scalar.copy(out=rounded[c][:, cols, :], in_=accs[c][b][:].rearrange("p t r -> p r t"))
                 else:
                     nc.vector.tensor_copy(out=rounded[c][:, cols, :], in_=accs[c][b][:].rearrange("p t r -> p r t"))
+                nc.scalar.copy(out=results[c][:, :, cols], in_=accs[c][b][:])
 
         def store_result(c):
             r0, n = starts[c], CHUNKS[c]
@@ -237,12 +246,14 @@ def tile_picked_yquadfm_max_po_kernel(
         units = [(c, t) for c in range(len(CHUNKS)) for t in range(PACK)]
         scalar_gathers(*units[0])
         for i, (c, t) in enumerate(units):
+            if c == 0 and 1 <= t < PACK - 1:
+                copy_out_y(t + 1, True)
             if i + 1 < len(units):
                 scalar_gathers(*units[i + 1])
             if c == 0:
                 scale_target(t)
-                if t + 2 < PACK:
-                    load_target(t + 2)
+                if t + 1 < PACK:
+                    load_target(t + 1)
             add_corners(c, t)
             if i > 0:
                 make_hid(*units[i - 1])

@@ -18,11 +18,13 @@ COPY = mybir.ActivationFunctionType.Copy
 
 P = 128
 PACK = 4
-BANK = 512
-STRIP = BANK // PACK
-CHUNKS = [512,384,128]
-WINDOW = max(S, max(CHUNKS)) + 16
-SCALAR_GATHERS = [[2,2,2,2],[2,2,2,3],[2,2,2,2]]
+QUADRANTS = 4
+PER_COLUMN = 16
+STRIP = 128
+HALF = S // 2
+CHUNKS = (512, 384, 128)
+SPAN = (2, 2, 1)
+WINDOW = S + PER_COLUMN
 
 
 def tile_picked_yquadfm_max_po_kernel(
@@ -34,6 +36,7 @@ def tile_picked_yquadfm_max_po_kernel(
         ring = ctx.enter_context(tc.tile_pool(name="ring", bufs=3))
         stage = ctx.enter_context(tc.tile_pool(name="stage", bufs=2))
         streamed = ctx.enter_context(tc.tile_pool(name="streamed", bufs=2))
+        pairs = ctx.enter_context(tc.tile_pool(name="pairs", bufs=2))
         psum = ctx.enter_context(tc.psum_pool(name="psum", bufs=8))
 
         def load_scale_rows(queue, plane, rows, q):
@@ -71,8 +74,8 @@ def tile_picked_yquadfm_max_po_kernel(
         w1_raw = streamed.tile([P, 2 * H], U8, name="streamed")
         x_word_table = streamed.tile([P, T], I32, name="streamed")
         weight_scale_rows = keep.tile([P, 2 * H], U8)
-        picks = keep.tile([P, S // 16], U16)
-        corners = [keep.tile([P, U // 16], U16, name="corner_%d" % i) for i in range(4)]
+        picks = keep.tile([P, S // PER_COLUMN], U16)
+        corners = [keep.tile([P, U // PER_COLUMN], U16, name="corner_%d" % i) for i in range(4)]
         nc.vector.memset(x_scale_table[:].bitcast(I32), 0)
         nc.vector.memset(weight_scale_rows[:].bitcast(I32), 0)
         nc.sync.dma_start(picks[:], offs)
@@ -80,23 +83,23 @@ def tile_picked_yquadfm_max_po_kernel(
             nc.sync.dma_start(corner[:], face_list)
         nc.sync.dma_start(out=w1_raw[:].bitcast(I32), in_=w1_words[0].bitcast(I32))
         nc.sync.dma_start(out=x_word_table[:], in_=x_words[0].rearrange("p c r -> p (c r)").bitcast(I32))
-        for q in range(4):
+        for q in range(QUADRANTS):
             load_scale_rows(nc.sync, x_scale_table[:], x_scales, q)
-        for q in range(4):
-            load_scale_rows(nc.gpsimd if q == 3 else nc.sync, weight_scale_rows[:, :H], w1_scales, q)
-        for q in range(4):
+        for q in range(QUADRANTS):
+            load_scale_rows(nc.gpsimd if q == QUADRANTS - 1 else nc.sync, weight_scale_rows[:, :H], w1_scales, q)
+        for q in range(QUADRANTS):
             load_scale_rows(nc.sync, weight_scale_rows[:, H:], w2_scales, q)
 
         starts = [sum(CHUNKS[:c]) for c in range(len(CHUNKS))]
+        last = len(CHUNKS) - 1
         tw_rows = tw.rearrange("(p t) r -> p t r", t=PACK)
         targets = []
+        scaled = []
 
         def load_target(t):
             target = streamed.tile([P, U], F32, name="streamed")
             nc.sync.dma_start(out=target[:], in_=tw_rows[:, t, :])
             targets.append(target)
-
-        scaled = []
 
         def scale_target(t):
             rows = keep.tile([P, U], F32, name="scaled_target_%d" % t)
@@ -107,20 +110,20 @@ def tile_picked_yquadfm_max_po_kernel(
         y = [keep.tile([P, WINDOW], F32, name="y_%d" % t) for t in range(PACK)]
         for t in range(PACK):
             nc.vector.memset(y[t][:, S:], 0.0)
-        half = S // 2
-        halves = [picks[:, h * half // 16 : (h + 1) * half // 16] for h in range(2)]
-        x_codes = [keep.tile([P, half], U32, align_bytes=64, name="x_codes_%d" % h) for h in range(2)]
-        x_code_scales = [keep.tile([P, half], U8, align_bytes=64, name="x_code_scales_%d" % h) for h in range(2)]
+        halves = [picks[:, h * HALF // PER_COLUMN : (h + 1) * HALF // PER_COLUMN] for h in range(2)]
+        x_codes = [keep.tile([P, HALF], U32, align_bytes=64, name="x_codes_%d" % h) for h in range(2)]
+        x_code_scales = [keep.tile([P, HALF], U8, align_bytes=64, name="x_code_scales_%d" % h) for h in range(2)]
         for h in range(2):
             nc.vector.tensor_copy(x_codes[h][:], x_word_table[:].bitcast(U32).indirect(halves[h]))
         nc.vector.tensor_copy(x_code_scales[0][:], x_scale_table[:].indirect(halves[0]))
         w1 = (w1_dealt, deal_scales(weight_scale_rows[:, :H], "w1_dealt_scales"))
         nc.vector.tensor_copy(x_code_scales[1][:], x_scale_table[:].indirect(halves[1]))
-        first = {}
+        y_banks = {}
         for h in range(2):
             for t in range(PACK):
-                first[h, t] = psum.tile([P, half], F32, name="acc")
-                product(first[h, t][:], w1, t, x_codes[h][:], x_code_scales[h][:])
+                y_banks[h, t] = psum.tile([P, HALF], F32, name="acc")
+                product(y_banks[h, t][:], w1, t, x_codes[h][:], x_code_scales[h][:])
+
         unit_cols = keep.tile([P, PACK], F32, name="unit_cols", tag="scale_table_then_unit")
         nc.sync.dma_start(out=unit_cols[:], in_=unit.rearrange("(p t) o -> p (t o)", t=PACK))
         w2_raw = streamed.tile([P, 2 * H], U8, name="streamed")
@@ -130,12 +133,13 @@ def tile_picked_yquadfm_max_po_kernel(
         def copy_out_y(t, on_scalar):
             for h in range(2):
                 if on_scalar:
-                    nc.scalar.activation(y[t][:, h * half : (h + 1) * half], first[h, t][:], COPY)
+                    nc.scalar.activation(y[t][:, h * HALF : (h + 1) * HALF], y_banks[h, t][:], COPY)
                 else:
-                    nc.vector.tensor_copy(out=y[t][:, h * half : (h + 1) * half], in_=first[h, t][:])
+                    nc.vector.tensor_copy(out=y[t][:, h * HALF : (h + 1) * HALF], in_=y_banks[h, t][:])
 
         copy_out_y(0, True)
         copy_out_y(1, False)
+        copy_out_y(2, False)
         w2 = (deal_words(w2_raw, "w2_dealt_words"), deal_scales(weight_scale_rows[:, H:], "w2_dealt_scales"))
 
         out_rows = out_0.rearrange("(p t) r -> p t r", t=PACK)
@@ -143,127 +147,131 @@ def tile_picked_yquadfm_max_po_kernel(
         plane_scales = keep.tile([P, U], U8, align_bytes=64)
 
         fetched = {}
+        sums = {}
+        larger = {}
         hid = {}
         grouped = {}
-        accs = {}
+        out_banks = {}
         results = {}
         rounded = {}
 
-        def window(c, t, which):
+        def looked_up(c, t, corner):
             r0, n = starts[c], CHUNKS[c]
-            return y[t][:].indirect(corners[which][:, r0 // 16 : (r0 + n) // 16])
+            return y[t][:].indirect(corners[corner][:, r0 // PER_COLUMN : (r0 + n) // PER_COLUMN])
 
-        def scalar_gathers(c, t):
-            n = CHUNKS[c]
-            for which in range(SCALAR_GATHERS[c][t]):
-                values = ring.tile([P, n], F32, name="fetched_%d" % which)
-                nc.scalar.activation(values[:], window(c, t, which), COPY)
-                fetched[c, t, which] = values
+        def fetch_corners(c, t):
+            for corner in range(2):
+                values = ring.tile([P, CHUNKS[c]], F32, name="fetched_%d" % corner)
+                nc.scalar.activation(values[:], looked_up(c, t, corner), COPY)
+                fetched[c, t, corner] = values
 
-        def diagonal(c, t, corner):
-            n = CHUNKS[c]
-            total = ring.tile([P, n], F32, name="diagonal_%d" % corner)
-            if (c, t, corner + 2) in fetched:
-                nc.vector.tensor_tensor(total[:], fetched[c, t, corner + 2][:], fetched[c, t, corner][:], ALU.add)
-            else:
-                nc.vector.tensor_tensor(total[:], window(c, t, corner + 2), fetched[c, t, corner][:], ALU.add)
-            return total
+        def add_opposite(c, t, corner):
+            if t % SPAN[c] == 0 and corner == 0:
+                sums[c, t // SPAN[c]] = [pairs.tile([P, SPAN[c], CHUNKS[c]], F32, name="diagonal_%d" % d) for d in range(2)]
+            total = sums[c, t // SPAN[c]][corner][:, t % SPAN[c], :]
+            nc.vector.tensor_tensor(total, looked_up(c, t, corner + 2), fetched[c, t, corner][:], ALU.add)
 
-        sums = {}
-        larger = {}
-
-        def add_corners(c, t):
-            sums[c, t] = (diagonal(c, t, 0), diagonal(c, t, 1))
+        def closes_group(c, t):
+            return (t + 1) % SPAN[c] == 0
 
         def take_larger(c, t):
-            larger[c, t] = ring.tile([P, CHUNKS[c]], F32, name="larger")
-            nc.vector.tensor_tensor(larger[c, t][:], sums[c, t][0][:], sums[c, t][1][:], ALU.max)
+            g = t // SPAN[c]
+            larger[c, g] = pairs.tile([P, SPAN[c], CHUNKS[c]], F32, name="larger")
+            nc.vector.tensor_tensor(larger[c, g][:], sums[c, g][0][:], sums[c, g][1][:], ALU.max)
 
         def make_hid(c, t):
             r0, n = starts[c], CHUNKS[c]
-            if t == 0:
-                hid[c] = stage.tile([P, PACK, n], BF16, name="hid")
-            nc.vector.scalar_tensor_tensor(
-                hid[c][:, t, :], larger[c, t][:], unit_cols[:, t : t + 1], scaled[t][:, r0 : r0 + n], ALU.mult, ALU.subtract
-            )
+            for j in range(t + 1 - SPAN[c], t + 1):
+                if j == 0:
+                    hid[c] = stage.tile([P, PACK, n], BF16, name="hid")
+                    grouped[c] = stage.tile([P, n, PACK], BF16, align_bytes=64, name="hid_grouped")
+                into = grouped[c][:, :, j] if (c, j) == (last, PACK - 1) else hid[c][:, j, :]
+                nc.vector.scalar_tensor_tensor(
+                    into, larger[c, j // SPAN[c]][:, j % SPAN[c], :], unit_cols[:, j : j + 1], scaled[j][:, r0 : r0 + n], ALU.mult, ALU.subtract
+                )
 
         def group_hid(c):
-            grouped[c] = stage.tile([P, CHUNKS[c], PACK], BF16, align_bytes=64, name="hid_grouped")
+            tiles = PACK - 1 if c == last else PACK
             nc.vector.tensor_copy(
-                out=grouped[c][:].rearrange("p (c i) t -> p c t i", i=4), in_=hid[c][:].rearrange("p t (c i) -> p c t i", i=4)
+                out=grouped[c][:, :, :tiles].rearrange("p (c i) t -> p c t i", i=4),
+                in_=hid[c][:, :tiles, :].rearrange("p t (c i) -> p c t i", i=4),
             )
+
+        def quantize(codes, scales, values):
+            nc.vector.quantize_mx(out=codes.bitcast(FP8X4), scales=scales, in_=values[:].rearrange("p r t -> p (r t)"))
 
         def second_product(c):
             n = CHUNKS[c]
             codes = stage.tile([P, n], U32, align_bytes=64, name="hid_codes")
             scales = stage.tile([P, n], U8, align_bytes=64, name="hid_scales")
-            nc.vector.quantize_mx(out=codes[:].bitcast(FP8X4), scales=scales[:], in_=grouped[c][:].rearrange("p r t -> p (r t)"))
-            accs[c] = []
+            quantize(codes[:], scales[:], grouped[c])
+            results[c] = stage.tile([P, PACK, n], F32, name="result")
+            rounded[c] = stage.tile([P, n, PACK], BF16, align_bytes=64, name="rounded")
+            out_banks[c] = []
             for b in range(n // STRIP):
                 acc = psum.tile([P, PACK, STRIP], F32, name="acc")
                 cols = slice(b * STRIP, (b + 1) * STRIP)
                 for t in range(PACK):
                     product(acc[:, t, :], w2, t, codes[:, cols], scales[:, cols])
-                accs[c].append(acc)
-            results[c] = stage.tile([P, PACK, n], F32, name="result")
-            rounded[c] = stage.tile([P, n, PACK], BF16, align_bytes=64, name="rounded")
+                out_banks[c].append(acc)
 
         def empty_banks(c, banks):
             for b in banks:
                 cols = slice(b * STRIP, (b + 1) * STRIP)
-                if c + 1 < len(CHUNKS):
-                    nc.scalar.copy(out=rounded[c][:, cols, :], in_=accs[c][b][:].rearrange("p t r -> p r t"))
-                else:
-                    nc.vector.tensor_copy(out=rounded[c][:, cols, :], in_=accs[c][b][:].rearrange("p t r -> p r t"))
-                nc.scalar.copy(out=results[c][:, :, cols], in_=accs[c][b][:])
+                nc.scalar.copy(out=rounded[c][:, cols, :], in_=out_banks[c][b][:].rearrange("p t r -> p r t"))
+                nc.scalar.copy(out=results[c][:, :, cols], in_=out_banks[c][b][:])
+                if b % 2 == 1 or b + 1 == len(out_banks[c]):
+                    j = b // 2 * 2 * STRIP
+                    nc.sync.dma_start(out=out_rows[:, :, starts[c] + j : starts[c] + cols.stop], in_=results[c][:, :, j : cols.stop])
 
-        def store_result(c):
-            r0, n = starts[c], CHUNKS[c]
-            nc.sync.dma_start(out=out_rows[:, :, r0 : r0 + n], in_=results[c][:])
+        def empty_last_bank():
+            nc.vector.tensor_copy(out=rounded[last][:], in_=out_banks[last][0][:].rearrange("p t r -> p r t"))
+            nc.scalar.copy(out=results[last][:], in_=out_banks[last][0][:])
+            nc.sync.dma_start(out=out_rows[:, :, starts[last] :], in_=results[last][:])
 
-        def store_planes(c):
+        def store_words(c):
             r0, n = starts[c], CHUNKS[c]
             words = stage.tile([P, n], I32, align_bytes=64, name="plane_words")
-            nc.vector.quantize_mx(
-                out=words[:].bitcast(FP8X4), scales=plane_scales[:, r0 : r0 + n], in_=rounded[c][:].rearrange("p r t -> p (r t)")
-            )
+            quantize(words[:], plane_scales[:, r0 : r0 + n], rounded[c])
             nc.sync.dma_start(out=out_words[:, r0 : r0 + n], in_=words[:])
 
-        def after_chunk(c, step):
-            banks = list(range(CHUNKS[c] // STRIP))
-            cut = (len(banks) + 1) // 2
-            if step == 0:
-                group_hid(c)
-            elif step == 1:
-                second_product(c)
-                empty_banks(c, banks[:cut])
-            elif step == 2:
-                empty_banks(c, banks[cut:])
-                store_result(c)
-            else:
-                store_planes(c)
-
         units = [(c, t) for c in range(len(CHUNKS)) for t in range(PACK)]
-        scalar_gathers(*units[0])
+        fetch_corners(*units[0])
         for i, (c, t) in enumerate(units):
-            if c == 0 and 1 <= t < PACK - 1:
-                copy_out_y(t + 1, True)
+            if (c, t) == (0, PACK - 2):
+                copy_out_y(PACK - 1, True)
             if i + 1 < len(units):
-                scalar_gathers(*units[i + 1])
+                fetch_corners(*units[i + 1])
             if c == 0:
                 scale_target(t)
                 if t + 1 < PACK:
                     load_target(t + 1)
-            add_corners(c, t)
-            if i > 0:
+            finished = i > 0 and closes_group(*units[i - 1])
+            banks = list(range(CHUNKS[c - 1] // STRIP))
+            cut = (len(banks) + 1) // 2
+            add_opposite(c, t, 0)
+            if finished:
+                take_larger(*units[i - 1])
+            if c > 0 and t == 1:
+                group_hid(c - 1)
+            add_opposite(c, t, 1)
+            if finished:
                 make_hid(*units[i - 1])
-            take_larger(c, t)
-            if c > 0:
-                after_chunk(c - 1, t)
+            if c > 0 and t == 1:
+                second_product(c - 1)
+                empty_banks(c - 1, banks[:cut])
+            if c > 0 and t == 2:
+                empty_banks(c - 1, banks[cut:])
+            if c > 1 and t == 0:
+                store_words(c - 2)
+        take_larger(*units[-1])
+        group_hid(last)
         make_hid(*units[-1])
-        for step in range(4):
-            after_chunk(len(CHUNKS) - 1, step)
-        for q in range(4):
-            nc.scalar.dma_start(
+        second_product(last)
+        store_words(last - 1)
+        empty_last_bank()
+        store_words(last)
+        for q in range(QUADRANTS):
+            (nc.scalar, nc.sync)[q % 2].dma_start(
                 out=out_2[0, 4 * q : 4 * q + 4, :].bitcast(I32), in_=plane_scales[32 * q : 32 * q + 4, :].bitcast(I32)
             )

@@ -218,11 +218,11 @@ def tile_picked_yquadfm_max_po_kernel(
         def empty_banks(c, banks):
             for b in banks:
                 cols = slice(b * STRIP, (b + 1) * STRIP)
-                nc.scalar.copy(out=rounded[c][:, cols, :], in_=out_banks[c][b][:].rearrange("p t r -> p r t"))
                 nc.scalar.copy(out=results[c][:, :, cols], in_=out_banks[c][b][:])
                 if b % 2 == 1 or b + 1 == len(out_banks[c]):
                     j = b // 2 * 2 * STRIP
                     nc.sync.dma_start(out=out_rows[:, :, starts[c] + j : starts[c] + cols.stop], in_=results[c][:, :, j : cols.stop])
+                nc.scalar.copy(out=rounded[c][:, cols, :], in_=out_banks[c][b][:].rearrange("p t r -> p r t"))
 
         def empty_last_bank():
             nc.vector.tensor_copy(out=rounded[last][:], in_=out_banks[last][0][:].rearrange("p t r -> p r t"))

from contextlib import ExitStack

import concourse.mybir as mybir

K, T, S, H, U = 512, 2048, 512, 512, 1024
FLOPS = 2 * K * H * S + 2 * H * H * U

F32 = mybir.dt.float32
BF16 = mybir.dt.bfloat16
I32 = mybir.dt.int32
U32 = mybir.dt.uint32
U16 = mybir.dt.uint16
U8 = mybir.dt.uint8
FP8X4 = mybir.dt.float8_e4m3fn_x4
FP4X4 = mybir.dt.float4_e2m1fn_x4
ALU = mybir.AluOpType
COPY = mybir.ActivationFunctionType.Copy

P = 128
PACK = 4
QUADRANTS = 4
PER_COLUMN = 16
STRIP = 128
HALF = S // 2
CHUNKS = (512, 384, 128)
SPAN = (2, 2, 1)
WINDOW = S + PER_COLUMN


def tile_picked_yquadfm_max_po_kernel(
    tc, x_words, x_scales, w1_words, w1_scales, tw, unit, w2_words, w2_scales, offs, f1, f2, f3, f4, out_0, out_1, out_2
):
    nc = tc.nc
    with ExitStack() as ctx:
        keep = ctx.enter_context(tc.tile_pool(name="keep", bufs=1))
        ring = ctx.enter_context(tc.tile_pool(name="ring", bufs=3))
        stage = ctx.enter_context(tc.tile_pool(name="stage", bufs=2))
        streamed = ctx.enter_context(tc.tile_pool(name="streamed", bufs=2))
        pairs = ctx.enter_context(tc.tile_pool(name="pairs", bufs=2))
        psum = ctx.enter_context(tc.psum_pool(name="psum", bufs=8))

        def load_scale_rows(queue, plane, rows, q):
            queue.dma_start(out=plane[32 * q : 32 * q + 4, :].bitcast(I32), in_=rows[0, 4 * q : 4 * q + 4, :].bitcast(I32))

        def deal_words(words, name):
            dealt = keep.tile([P, 2 * H], U8, align_bytes=64, name=name)
            nc.vector.tensor_copy(
                out=dealt[:].rearrange("p (t m b) -> p t m b", t=PACK, b=2),
                in_=words[:].rearrange("p (m t b) -> p t m b", t=PACK, b=2),
            )
            return dealt

        def deal_scales(scales, name):
            dealt = keep.tile([P, H], U8, align_bytes=64, name=name)
            nc.vector.tensor_copy(
                out=dealt[:].rearrange("p (t m) -> p t m", t=PACK),
                in_=scales.rearrange("p (m t) -> p t m", t=PACK),
            )
            return dealt

        def product(acc, weights, t, codes, scales):
            words, weight_scales = weights
            nc.tensor.matmul_mx(
                out=acc,
                lhsT=words[:, 2 * P * t : 2 * P * (t + 1)].bitcast(FP4X4),
                lhsT_scale=weight_scales[:, P * t : P * (t + 1)],
                rhs=codes.bitcast(FP8X4),
                rhs_scale=scales,
                start=True,
                stop=True,
            )

        x_scale_table = keep.tile([P, T], U8, name="x_scale_table", tag="scale_table_then_unit")
        w1_raw = streamed.tile([P, 2 * H], U8, name="streamed")
        x_word_table = streamed.tile([P, T], I32, name="streamed")
        weight_scale_rows = keep.tile([P, 2 * H], U8)
        picks = keep.tile([P, S // PER_COLUMN], U16)
        corners = [keep.tile([P, U // PER_COLUMN], U16, name="corner_%d" % i) for i in range(4)]
        nc.vector.memset(x_scale_table[:].bitcast(I32), 0)
        nc.vector.memset(weight_scale_rows[:].bitcast(I32), 0)
        nc.sync.dma_start(picks[:], offs)
        for corner, face_list in zip(corners, (f1, f2, f3, f4)):
            nc.sync.dma_start(corner[:], face_list)
        nc.sync.dma_start(out=w1_raw[:].bitcast(I32), in_=w1_words[0].bitcast(I32))
        nc.sync.dma_start(out=x_word_table[:], in_=x_words[0].rearrange("p c r -> p (c r)").bitcast(I32))
        for q in range(QUADRANTS):
            load_scale_rows(nc.sync, x_scale_table[:], x_scales, q)
        for q in range(QUADRANTS):
            load_scale_rows(nc.gpsimd if q == QUADRANTS - 1 else nc.sync, weight_scale_rows[:, :H], w1_scales, q)
        for q in range(QUADRANTS):
            load_scale_rows(nc.sync, weight_scale_rows[:, H:], w2_scales, q)

        starts = [sum(CHUNKS[:c]) for c in range(len(CHUNKS))]
        last = len(CHUNKS) - 1
        tw_rows = tw.rearrange("(p t) r -> p t r", t=PACK)
        targets = []
        scaled = []

        def load_target(t):
            target = streamed.tile([P, U], F32, name="streamed")
            nc.sync.dma_start(out=target[:], in_=tw_rows[:, t, :])
            targets.append(target)

        def scale_target(t):
            rows = keep.tile([P, U], F32, name="scaled_target_%d" % t)
            nc.scalar.activation(rows[:], targets[t][:], COPY, scale=unit_cols[:, t : t + 1])
            scaled.append(rows)

        w1_dealt = deal_words(w1_raw, "w1_dealt_words")
        y = [keep.tile([P, WINDOW], F32, name="y_%d" % t) for t in range(PACK)]
        for t in range(PACK):
            nc.vector.memset(y[t][:, S:], 0.0)
        halves = [picks[:, h * HALF // PER_COLUMN : (h + 1) * HALF // PER_COLUMN] for h in range(2)]
        x_codes = [keep.tile([P, HALF], U32, align_bytes=64, name="x_codes_%d" % h) for h in range(2)]
        x_code_scales = [keep.tile([P, HALF], U8, align_bytes=64, name="x_code_scales_%d" % h) for h in range(2)]
        for h in range(2):
            nc.vector.tensor_copy(x_codes[h][:], x_word_table[:].bitcast(U32).indirect(halves[h]))
        nc.vector.tensor_copy(x_code_scales[0][:], x_scale_table[:].indirect(halves[0]))
        w1 = (w1_dealt, deal_scales(weight_scale_rows[:, :H], "w1_dealt_scales"))
        nc.vector.tensor_copy(x_code_scales[1][:], x_scale_table[:].indirect(halves[1]))
        y_banks = {}
        for h in range(2):
            for t in range(PACK):
                y_banks[h, t] = psum.tile([P, HALF], F32, name="acc")
                product(y_banks[h, t][:], w1, t, x_codes[h][:], x_code_scales[h][:])

        unit_cols = keep.tile([P, PACK], F32, name="unit_cols", tag="scale_table_then_unit")
        nc.sync.dma_start(out=unit_cols[:], in_=unit.rearrange("(p t) o -> p (t o)", t=PACK))
        w2_raw = streamed.tile([P, 2 * H], U8, name="streamed")
        nc.sync.dma_start(out=w2_raw[:].bitcast(I32), in_=w2_words[0].bitcast(I32))
        load_target(0)

        def copy_out_y(t, on_scalar):
            for h in range(2):
                if on_scalar:
                    nc.scalar.activation(y[t][:, h * HALF : (h + 1) * HALF], y_banks[h, t][:], COPY)
                else:
                    nc.vector.tensor_copy(out=y[t][:, h * HALF : (h + 1) * HALF], in_=y_banks[h, t][:])

        copy_out_y(0, True)
        copy_out_y(1, False)
        copy_out_y(2, False)
        w2 = (deal_words(w2_raw, "w2_dealt_words"), deal_scales(weight_scale_rows[:, H:], "w2_dealt_scales"))

        out_rows = out_0.rearrange("(p t) r -> p t r", t=PACK)
        out_words = out_1[0].rearrange("p c r -> p (c r)").bitcast(I32)
        plane_scales = keep.tile([P, U], U8, align_bytes=64)

        fetched = {}
        sums = {}
        larger = {}
        hid = {}
        grouped = {}
        out_banks = {}
        results = {}
        rounded = {}

        def looked_up(c, t, corner):
            r0, n = starts[c], CHUNKS[c]
            return y[t][:].indirect(corners[corner][:, r0 // PER_COLUMN : (r0 + n) // PER_COLUMN])

        def fetch_corners(c, t):
            for corner in range(2):
                values = ring.tile([P, CHUNKS[c]], F32, name="fetched_%d" % corner)
                nc.scalar.activation(values[:], looked_up(c, t, corner), COPY)
                fetched[c, t, corner] = values

        def add_opposite(c, t, corner):
            if t % SPAN[c] == 0 and corner == 0:
                sums[c, t // SPAN[c]] = [pairs.tile([P, SPAN[c], CHUNKS[c]], F32, name="diagonal_%d" % d) for d in range(2)]
            total = sums[c, t // SPAN[c]][corner][:, t % SPAN[c], :]
            nc.vector.tensor_tensor(total, looked_up(c, t, corner + 2), fetched[c, t, corner][:], ALU.add)

        def closes_group(c, t):
            return (t + 1) % SPAN[c] == 0

        def take_larger(c, t):
            g = t // SPAN[c]
            larger[c, g] = pairs.tile([P, SPAN[c], CHUNKS[c]], F32, name="larger")
            nc.vector.tensor_tensor(larger[c, g][:], sums[c, g][0][:], sums[c, g][1][:], ALU.max)

        def make_hid(c, t):
            r0, n = starts[c], CHUNKS[c]
            for j in range(t + 1 - SPAN[c], t + 1):
                if j == 0:
                    hid[c] = stage.tile([P, PACK, n], BF16, name="hid")
                    grouped[c] = stage.tile([P, n, PACK], BF16, align_bytes=64, name="hid_grouped")
                into = grouped[c][:, :, j] if (c, j) == (last, PACK - 1) else hid[c][:, j, :]
                nc.vector.scalar_tensor_tensor(
                    into, larger[c, j // SPAN[c]][:, j % SPAN[c], :], unit_cols[:, j : j + 1], scaled[j][:, r0 : r0 + n], ALU.mult, ALU.subtract
                )

        def group_hid(c):
            tiles = PACK - 1 if c == last else PACK
            nc.vector.tensor_copy(
                out=grouped[c][:, :, :tiles].rearrange("p (c i) t -> p c t i", i=4),
                in_=hid[c][:, :tiles, :].rearrange("p t (c i) -> p c t i", i=4),
            )

        def quantize(codes, scales, values):
            nc.vector.quantize_mx(out=codes.bitcast(FP8X4), scales=scales, in_=values[:].rearrange("p r t -> p (r t)"))

        def second_product(c):
            n = CHUNKS[c]
            codes = stage.tile([P, n], U32, align_bytes=64, name="hid_codes")
            scales = stage.tile([P, n], U8, align_bytes=64, name="hid_scales")
            quantize(codes[:], scales[:], grouped[c])
            results[c] = stage.tile([P, PACK, n], F32, name="result")
            rounded[c] = stage.tile([P, n, PACK], BF16, align_bytes=64, name="rounded")
            out_banks[c] = []
            for b in range(n // STRIP):
                acc = psum.tile([P, PACK, STRIP], F32, name="acc")
                cols = slice(b * STRIP, (b + 1) * STRIP)
                for t in range(PACK):
                    product(acc[:, t, :], w2, t, codes[:, cols], scales[:, cols])
                out_banks[c].append(acc)

        def empty_banks(c, banks):
            for b in banks:
                cols = slice(b * STRIP, (b + 1) * STRIP)
                nc.scalar.copy(out=results[c][:, :, cols], in_=out_banks[c][b][:])
                if b % 2 == 1 or b + 1 == len(out_banks[c]):
                    j = b // 2 * 2 * STRIP
                    nc.sync.dma_start(out=out_rows[:, :, starts[c] + j : starts[c] + cols.stop], in_=results[c][:, :, j : cols.stop])
                nc.scalar.copy(out=rounded[c][:, cols, :], in_=out_banks[c][b][:].rearrange("p t r -> p r t"))

        def empty_last_bank():
            nc.vector.tensor_copy(out=rounded[last][:], in_=out_banks[last][0][:].rearrange("p t r -> p r t"))
            nc.scalar.copy(out=results[last][:], in_=out_banks[last][0][:])
            nc.sync.dma_start(out=out_rows[:, :, starts[last] :], in_=results[last][:])

        def store_words(c):
            r0, n = starts[c], CHUNKS[c]
            words = stage.tile([P, n], I32, align_bytes=64, name="plane_words")
            quantize(words[:], plane_scales[:, r0 : r0 + n], rounded[c])
            nc.sync.dma_start(out=out_words[:, r0 : r0 + n], in_=words[:])

        units = [(c, t) for c in range(len(CHUNKS)) for t in range(PACK)]
        fetch_corners(*units[0])
        for i, (c, t) in enumerate(units):
            if (c, t) == (0, PACK - 2):
                copy_out_y(PACK - 1, True)
            if i + 1 < len(units):
                fetch_corners(*units[i + 1])
            if c == 0:
                scale_target(t)
                if t + 1 < PACK:
                    load_target(t + 1)
            finished = i > 0 and closes_group(*units[i - 1])
            banks = list(range(CHUNKS[c - 1] // STRIP))
            cut = (len(banks) + 1) // 2
            add_opposite(c, t, 0)
            if finished:
                take_larger(*units[i - 1])
            if c > 0 and t == 1:
                group_hid(c - 1)
            add_opposite(c, t, 1)
            if finished:
                make_hid(*units[i - 1])
            if c > 0 and t == 1:
                second_product(c - 1)
                empty_banks(c - 1, banks[:cut])
            if c > 0 and t == 2:
                empty_banks(c - 1, banks[cut:])
            if c > 1 and t == 0:
                store_words(c - 2)
        take_larger(*units[-1])
        group_hid(last)
        make_hid(*units[-1])
        second_product(last)
        store_words(last - 1)
        empty_last_bank()
        store_words(last)
        for q in range(QUADRANTS):
            (nc.scalar, nc.sync)[q % 2].dma_start(
                out=out_2[0, 4 * q : 4 * q + 4, :].bitcast(I32), in_=plane_scales[32 * q : 32 * q + 4, :].bitcast(I32)
            )
